import numpy as np
import ml_dtypes


def mxq(x, axis, fmt="e4m3"):
    dtype, down = {"e4m3": (ml_dtypes.float8_e4m3fn, 7), "e5m2": (ml_dtypes.float8_e5m2, 14)}[fmt]
    v = np.moveaxis(np.asarray(x, np.float32).astype(ml_dtypes.bfloat16).astype(np.float64), axis, -1)
    blocks = v.reshape(v.shape[:-1] + (-1, 32))
    amax = np.abs(blocks).max(-1, keepdims=True)
    byte = np.maximum(np.where(amax > 0, np.frexp(amax)[1] - 1 + 127, 0) - down, 1)
    scale = np.exp2(byte - 127.0)
    codes = (blocks / scale).astype(np.float32).astype(dtype).astype(np.float64)
    return np.moveaxis((codes * scale).reshape(v.shape), -1, axis)


WIDE = False


def mx_kscale(k):
    if not WIDE:
        return np.ones(k)
    levels = np.array([18, -18])
    if k % 512:
        return np.exp2(np.random.permutation(np.resize(levels, k // 32))).repeat(32)
    a = np.empty((k // 512, 16))
    for p in range(k // 512):
        a[p, :8] = np.random.permutation(np.resize(levels, 8))
        for g in range(8):
            far = levels[np.abs(levels - a[p, g]) >= 10]
            a[p, g + 8] = far[np.random.randint(len(far))]
    return np.exp2(a.ravel()).repeat(32)


def f64(x):
    return np.asarray(x).astype(np.float64)


def striped(idx):
    return np.tile(np.asarray(idx).reshape(-1, 16).T, (8, 1)).astype(np.uint16)


def unstriped(offs):
    return offs[:16].T.reshape(-1).astype(np.int64)


def clip(x, c):
    return np.minimum(np.maximum(x, -c), c)


def setup_inputs():
    n = np.random.standard_normal
    uni = np.random.uniform
    idx = np.random.permutation(2048)[:512]
    f_d = mx_kscale(512)
    return {
        "xT": (n((512, 512)) * f_d[:, None]).astype(np.float32),
        "wT": (n((512, 2048)) / np.sqrt(512) / f_d[:, None]).astype(np.float32),
        "ts": np.tile(uni(0.75, 1.3, 2048), (128, 1)).astype(np.float32),
        "kb": np.tile(0.5 * n(2048), (128, 1)).astype(np.float32),
        "us": (uni(0.75, 1.3, (512, 1))).astype(np.float32),
        "y": (n((512, 512))).astype(np.float32),
        "wt": (uni(0.75, 1.3, (512, 1)) / np.sqrt(512)).astype(np.float32),
        "offs": striped(idx),
    }


def reference(xT, wT, ts, kb, us, y, wt, offs):
    idx = unstriped(offs)
    wT_i = f64(wT)[:, idx]
    ts_i = f64(ts)[:1][:, idx]
    kb_i = f64(kb)[:1][:, idx]
    a = mxq(f64(xT), 0, "e4m3").T @ mxq(wT_i, 0, "e4m3")
    z = f64(us) * ts_i * a + kb_i
    g = f64(wt) * clip(z - f64(y), 1.0)
    q = g * f64(us) * a
    qt = q.T
    ds = (qt).sum(-1, keepdims=True)
    out_0 = ds.T
    gt = g.T
    db = (gt).sum(-1, keepdims=True)
    out_1 = db.T
    du = (g * ts_i * a).sum(-1, keepdims=True)
    out_2 = du.T
    return out_0, out_1, out_2

@@ -1,0 +1,187 @@
+from contextlib import ExitStack
+
+import concourse.mybir as mybir
+from concourse.masks import make_identity
+
+F32 = mybir.dt.float32
+BF16 = mybir.dt.bfloat16
+U32 = mybir.dt.uint32
+U16 = mybir.dt.uint16
+U8 = mybir.dt.uint8
+FP8X4 = mybir.dt.float8_e4m3fn_x4
+ALU = mybir.AluOpType
+ACT = mybir.ActivationFunctionType
+AXIS = mybir.AxisListType
+
+P = 128
+PACK = 4
+D, R, SLOTS, COLS = 512, 512, 512, 2048
+TILES = R // P
+BLOCKS = SLOTS // P
+HALF = 256
+FLOPS = 2 * D * R * SLOTS
+BYTES = 4 * (D * R + D * COLS + 2 * COLS + 2 * R + R * SLOTS + 2 * SLOTS + R) + 2 * 128 * 32
+
+
+def tile_attend_gbias_s_hub_kernel(tc, xT, wT, ts, kb, us, y, wt, offs, out_0, out_1, out_2):
+    nc = tc.nc
+    with ExitStack() as ctx:
+        held = ctx.enter_context(tc.tile_pool(name="held", bufs=1))
+        psum = ctx.enter_context(tc.psum_pool(name="psum", bufs=1))
+
+        offsets = held.tile([P, SLOTS // 16], U16, name="offsets")
+        nc.sync.dma_start(offsets[:], offs)
+
+        ts_row = held.tile([1, COLS], F32, name="ts_staged")
+        kb_row = held.tile([1, COLS], F32, name="kb_staged")
+        nc.sync.dma_start(ts_row[:], ts[0:1, :])
+        nc.sync.dma_start(kb_row[:], kb[0:1, :])
+
+        w_rows = wT.rearrange("(p t) c -> t p c", t=PACK)
+        w_plane = [held.tile([P, COLS], F32, name=f"w_plane{t}") for t in range(PACK)]
+        for t in range(PACK):
+            nc.sync.dma_start(w_plane[t][:], w_rows[t])
+
+        ts_window = held.tile([P, COLS], F32, name="ts_window")
+        kb_window = held.tile([P, COLS], F32, name="kb_window")
+        for window, staged in ((ts_window, ts_row), (kb_window, kb_row)):
+            nc.vector.memset(window[:], 0.0)
+            nc.scalar.activation(window[0:1, :], staged[:], ACT.Copy)
+
+        us_col = held.tile([P, TILES], F32, name="us_col")
+        wt_col = held.tile([P, TILES], F32, name="wt_col")
+        with nc.allow_non_contiguous_dma(reason="one value a row tile and partition"):
+            nc.sync.dma_start(us_col[:], us.rearrange("(n p) o -> p n o", p=P)[:, :, 0])
+            nc.sync.dma_start(wt_col[:], wt.rearrange("(n p) o -> p n o", p=P)[:, :, 0])
+
+        x_rows = xT.rearrange("(p t) r -> p t r", t=PACK)
+        y_rows = y.rearrange("(n p) i -> p n i", p=P)
+        x_half = [held.tile([P, PACK, HALF], F32, name=f"x_half{h}") for h in range(2)]
+        y_half = [held.tile([P, 2, SLOTS], F32, name=f"y_half{h}") for h in range(2)]
+        for h in range(2):
+            nc.sync.dma_start(x_half[h][:], x_rows[:, :, h * HALF : (h + 1) * HALF])
+            nc.sync.dma_start(y_half[h][:], y_rows[:, 2 * h : 2 * h + 2, :])
+
+        ident = held.tile([P, P], F32, name="ident")
+        make_identity(nc, ident[:])
+        stats = held.tile([P, P], F32, name="stats", align_bytes=64)
+        nc.gpsimd.memset(stats[:], 0.0)
+
+        def spread(window, name):
+            row = held.tile([P, SLOTS], F32, name=name + "_row")
+            nc.vector.tensor_copy(row[:], window[:].indirect(offsets[:]))
+            turned = psum.tile([P, BLOCKS, P], F32, name=name + "_turned", tag="turned")
+            for j in range(BLOCKS):
+                nc.tensor.transpose(turned[:, j, :], row[:, j * P : (j + 1) * P], ident[:])
+            col = held.tile([P, BLOCKS], F32, name=name + "_col")
+            nc.scalar.copy(col[:], turned[:, :, 0])
+            back = psum.tile([P, BLOCKS, P], F32, name=name + "_back", tag="back")
+            for j in range(BLOCKS):
+                nc.tensor.transpose(back[:, j, :], col[:, j : j + 1].to_broadcast([P, P]), ident[:])
+            full = held.tile([P, SLOTS], F32, name=name + "_all")
+            nc.scalar.copy(full[:], back[:].rearrange("p j s -> p (j s)"))
+            return full
+
+        ts_all = spread(ts_window, "ts")
+        kb_all = spread(kb_window, "kb")
+
+        wu_col = held.tile([P, TILES], F32, name="wu_col")
+        nc.gpsimd.tensor_tensor(wu_col[:], us_col[:], wt_col[:], ALU.mult)
+
+        w_words = held.tile([P, SLOTS, PACK], BF16, name="w_words", align_bytes=64)
+        for t in range(PACK - 1):
+            nc.vector.tensor_copy(w_words[:, :, t], w_plane[t][:].indirect(offsets[:]))
+        w_codes = held.tile([P, SLOTS], U32, name="w_codes", align_bytes=64)
+        w_scales = held.tile([P, SLOTS], U8, name="w_scales", align_bytes=64)
+        for h in range(2):
+            nc.vector.tensor_copy(
+                w_words[:, h * HALF : (h + 1) * HALF, PACK - 1],
+                w_plane[PACK - 1][:].indirect(offsets[:, h * (HALF // 16) : (h + 1) * (HALF // 16)]),
+            )
+        for h in range(2):
+            cols = slice(h * HALF, (h + 1) * HALF)
+            nc.vector.quantize_mx(
+                w_codes[:, cols].bitcast(FP8X4), w_scales[:, cols], w_words[:, cols, :].rearrange("p s t -> p (s t)")
+            )
+
+        a_bank = []
+        for n in range(TILES):
+            x_words = held.tile([P, P, PACK], BF16, name=f"x_words{n}", align_bytes=64)
+            source = x_half[n // 2][:, :, (n % 2) * P : (n % 2 + 1) * P]
+            nc.scalar.copy(
+                x_words[:].rearrange("p (c i) t -> p c t i", i=4), source.rearrange("p t (c i) -> p c t i", i=4)
+            )
+            x_codes = held.tile([P, P], U32, name=f"x_codes{n}", align_bytes=64)
+            x_scales = held.tile([P, P], U8, name=f"x_scales{n}", align_bytes=64)
+            nc.vector.quantize_mx(x_codes[:].bitcast(FP8X4), x_scales[:], x_words[:].rearrange("p r t -> p (r t)"))
+            bank = psum.tile([P, SLOTS], F32, name=f"a_bank{n}")
+            nc.tensor.matmul_mx(
+                bank[:],
+                lhsT=x_codes[:].bitcast(FP8X4),
+                lhsT_scale=x_scales[:],
+                rhs=w_codes[:].bitcast(FP8X4),
+                rhs_scale=w_scales[:],
+                start=True,
+                stop=True,
+            )
+            a_bank.append(bank)
+
+        ds_sum = psum.tile([P, BLOCKS, P], F32, name="ds_sum")
+        db_sum = psum.tile([P, BLOCKS, P], F32, name="db_sum")
+
+        def add_turned(total, tile, n):
+            for j in range(BLOCKS):
+                nc.tensor.matmul(
+                    total[:, j, :],
+                    lhsT=tile[:, j * P : (j + 1) * P],
+                    rhs=ident[:],
+                    is_transpose=True,
+                    start=(n == 0 and j == 0),
+                    stop=(n == TILES - 1 and j == BLOCKS - 1),
+                )
+
+        ta = [held.tile([P, SLOTS], F32, name=f"ta{n}") for n in range(TILES)]
+        clipped = [held.tile([P, SLOTS], F32, name=f"clipped{n}") for n in range(TILES)]
+
+        def front(n):
+            target = held.tile([P, SLOTS], F32, name=f"target{n}")
+            nc.gpsimd.tensor_tensor(target[:], y_half[n // 2][:, n % 2, :], kb_all[:], ALU.subtract)
+            nc.vector.tensor_tensor(ta[n][:], a_bank[n][:], ts_all[:], ALU.mult)
+            err = held.tile([P, SLOTS], F32, name=f"err{n}")
+            nc.vector.scalar_tensor_tensor(err[:], ta[n][:], us_col[:, n : n + 1], target[:], ALU.mult, ALU.subtract)
+            nc.vector.tensor_scalar(clipped[n][:], err[:], 1.0, -1.0, ALU.min, ALU.max)
+
+        def back_half(n):
+            g = held.tile([P, SLOTS], F32, name=f"g{n}")
+            nc.scalar.activation(g[:], clipped[n][:], ACT.Copy, scale=wt_col[:, n : n + 1])
+            add_turned(db_sum, g, n)
+            q = held.tile([P, SLOTS], F32, name=f"q{n}")
+            nc.vector.scalar_tensor_tensor(q[:], clipped[n][:], wu_col[:, n : n + 1], a_bank[n][:], ALU.mult, ALU.mult)
+            add_turned(ds_sum, q, n)
+            gta = held.tile([P, SLOTS], F32, name=f"gta{n}")
+            nc.vector.scalar_tensor_tensor(
+                gta[:],
+                clipped[n][:],
+                wt_col[:, n : n + 1],
+                ta[n][:],
+                ALU.mult,
+                ALU.mult,
+                accum_out=stats[:, 32 * n + 2 : 32 * n + 3],
+            )
+
+        front(0)
+        for n in range(1, TILES):
+            front(n)
+            back_half(n - 1)
+        back_half(TILES - 1)
+
+        by_block = stats[:].rearrange("p (j c) -> p j c", c=32)
+        nc.vector.tensor_reduce(by_block[:, :, 1], db_sum[:], AXIS.X, ALU.add)
+        nc.vector.tensor_reduce(by_block[:, :, 0], ds_sum[:], AXIS.X, ALU.add)
+        rows = held.tile([P, P], F32, name="rows", align_bytes=64)
+        nc.vector.transpose(rows[:], stats[:])
+        for o, (out, queue) in enumerate(((out_0, nc.sync), (out_1, nc.scalar), (out_2, nc.sync))):
+            queue.dma_start(
+                out.rearrange("o (j b k) -> b (o j) k", b=4, k=32),
+                rows[o:P:32, :].rearrange("b (j k) -> b j k", k=32),
+            )

@@ -37,6 +37,10 @@ def tile_attend_gbias_s_hub_kernel(tc, xT, wT, ts, kb, us, y, wt, offs, out_0, o
         nc.sync.dma_start(ts_row[:], ts[0:1, :])
         nc.sync.dma_start(kb_row[:], kb[0:1, :])
 
+        row_scales = held.tile([P, R], F32, name="row_scales")
+        nc.sync.dma_start(row_scales[32:33, :], us.rearrange("r o -> o r"))
+        nc.sync.dma_start(row_scales[64:65, :], wt.rearrange("r o -> o r"))
+
         w_rows = wT.rearrange("(p t) c -> t p c", t=PACK)
         w_plane = [held.tile([P, COLS], F32, name=f"w_plane{t}") for t in range(PACK)]
         for t in range(PACK):
@@ -44,15 +48,15 @@ def tile_attend_gbias_s_hub_kernel(tc, xT, wT, ts, kb, us, y, wt, offs, out_0, o
 
         ts_window = held.tile([P, COLS], F32, name="ts_window")
         kb_window = held.tile([P, COLS], F32, name="kb_window")
-        for window, staged in ((ts_window, ts_row), (kb_window, kb_row)):
-            nc.vector.memset(window[:], 0.0)
-            nc.scalar.activation(window[0:1, :], staged[:], ACT.Copy)
+        one = held.tile([P, 1], F32, name="one")
+        two = held.tile([P, 1], F32, name="two")
+        nc.gpsimd.memset(one[:], 1.0)
+        nc.scalar.activation(two[:], one[:], ACT.Identity, bias=one[:])
+        nc.vector.memset(ts_window[:], 0.0)
+        nc.gpsimd.memset(kb_window[:], 0.0)
+        nc.vector.tensor_copy(ts_window[0:1, :], ts_row[:])
+        nc.scalar.activation(kb_window[0:1, :], kb_row[:], ACT.Copy)
 
-        us_col = held.tile([P, TILES], F32, name="us_col")
-        wt_col = held.tile([P, TILES], F32, name="wt_col")
-        with nc.allow_non_contiguous_dma(reason="one value a row tile and partition"):
-            nc.sync.dma_start(us_col[:], us.rearrange("(n p) o -> p n o", p=P)[:, :, 0])
-            nc.sync.dma_start(wt_col[:], wt.rearrange("(n p) o -> p n o", p=P)[:, :, 0])
 
         x_rows = xT.rearrange("(p t) r -> p t r", t=PACK)
         y_rows = y.rearrange("(n p) i -> p n i", p=P)
@@ -67,26 +71,38 @@ def tile_attend_gbias_s_hub_kernel(tc, xT, wT, ts, kb, us, y, wt, offs, out_0, o
         stats = held.tile([P, P], F32, name="stats", align_bytes=64)
         nc.gpsimd.memset(stats[:], 0.0)
 
-        def spread(window, name):
+        def gathered_row(window, name):
             row = held.tile([P, SLOTS], F32, name=name + "_row")
             nc.vector.tensor_copy(row[:], window[:].indirect(offsets[:]))
+            return row
+
+        def columns(row, name, picked):
             turned = psum.tile([P, BLOCKS, P], F32, name=name + "_turned", tag="turned")
             for j in range(BLOCKS):
                 nc.tensor.transpose(turned[:, j, :], row[:, j * P : (j + 1) * P], ident[:])
-            col = held.tile([P, BLOCKS], F32, name=name + "_col")
-            nc.scalar.copy(col[:], turned[:, :, 0])
-            back = psum.tile([P, BLOCKS, P], F32, name=name + "_back", tag="back")
+            col = held.tile([P, picked, BLOCKS], F32, name=name + "_col")
+            nc.scalar.copy(col[:], turned[:, :, 0 : 32 * picked : 32].rearrange("p j c -> p c j"))
+            return col
+
+        def spread(col, name, tag):
+            back = psum.tile([P, SLOTS], F32, name=name + "_back", tag=tag)
             for j in range(BLOCKS):
-                nc.tensor.transpose(back[:, j, :], col[:, j : j + 1].to_broadcast([P, P]), ident[:])
-            full = held.tile([P, SLOTS], F32, name=name + "_all")
-            nc.scalar.copy(full[:], back[:].rearrange("p j s -> p (j s)"))
-            return full
+                nc.tensor.transpose(back[:, j * P : (j + 1) * P], col[:, j : j + 1].to_broadcast([P, P]), ident[:])
+            return back
 
-        ts_all = spread(ts_window, "ts")
-        kb_all = spread(kb_window, "kb")
-
+        ts_picked = gathered_row(ts_window, "ts")
+        for part in (32, 64):
+            nc.scalar.copy(ts_picked[part : part + 1, :], row_scales[part : part + 1, :])
+        cols_held = columns(ts_picked, "ts", 3)
+        us_col = cols_held[:, 1, :]
+        wt_col = cols_held[:, 2, :]
+        ts_all = held.tile([P, SLOTS], F32, name="ts_all")
+        nc.scalar.copy(ts_all[:], spread(cols_held[:, 0, :], "ts", "ds_sum")[:])
+        kb_all = spread(columns(gathered_row(kb_window, "kb"), "kb", 1)[:, 0, :], "kb", "kb_all")
         wu_col = held.tile([P, TILES], F32, name="wu_col")
-        nc.gpsimd.tensor_tensor(wu_col[:], us_col[:], wt_col[:], ALU.mult)
+        nc.gpsimd.tensor_tensor(wu_col[:], us_col, wt_col, ALU.mult)
+        minus_wt = held.tile([P, TILES], F32, name="minus_wt")
+        nc.gpsimd.tensor_scalar(minus_wt[:], wt_col, -1.0, 0.0, ALU.mult, ALU.add)
 
         w_words = held.tile([P, SLOTS, PACK], BF16, name="w_words", align_bytes=64)
         for t in range(PACK - 1):
@@ -141,42 +157,73 @@ def tile_attend_gbias_s_hub_kernel(tc, xT, wT, ts, kb, us, y, wt, offs, out_0, o
                 )
 
         ta = [held.tile([P, SLOTS], F32, name=f"ta{n}") for n in range(TILES)]
+        g = [held.tile([P, SLOTS], F32, name=f"g{n}") for n in range(TILES)]
         clipped = [held.tile([P, SLOTS], F32, name=f"clipped{n}") for n in range(TILES)]
+        ON_SCALAR = (1, 2)
 
-        def front(n):
-            target = held.tile([P, SLOTS], F32, name=f"target{n}")
-            nc.gpsimd.tensor_tensor(target[:], y_half[n // 2][:, n % 2, :], kb_all[:], ALU.subtract)
+        err = [held.tile([P, SLOTS], F32, name=f"err{n}") for n in range(TILES)]
+
+        def make_ta(n):
             nc.vector.tensor_tensor(ta[n][:], a_bank[n][:], ts_all[:], ALU.mult)
-            err = held.tile([P, SLOTS], F32, name=f"err{n}")
-            nc.vector.scalar_tensor_tensor(err[:], ta[n][:], us_col[:, n : n + 1], target[:], ALU.mult, ALU.subtract)
-            nc.vector.tensor_scalar(clipped[n][:], err[:], 1.0, -1.0, ALU.min, ALU.max)
 
-        def back_half(n):
-            g = held.tile([P, SLOTS], F32, name=f"g{n}")
-            nc.scalar.activation(g[:], clipped[n][:], ACT.Copy, scale=wt_col[:, n : n + 1])
-            add_turned(db_sum, g, n)
+        def make_err(n):
+            z = held.tile([P, SLOTS], F32, name=f"z{n}")
+            nc.vector.scalar_tensor_tensor(z[:], ta[n][:], us_col[:, n : n + 1], kb_all[:], ALU.mult, ALU.add)
+            nc.gpsimd.tensor_tensor(err[n][:], z[:], y_half[n // 2][:, n % 2, :], ALU.subtract)
+
+        def clip(n):
+            if n in ON_SCALAR:
+                low = held.tile([P, SLOTS], F32, name=f"low{n}")
+                nc.scalar.activation(low[:], err[n][:], ACT.Relu, bias=one[:])
+                nc.scalar.activation(clipped[n][:], low[:], ACT.Relu, scale=-1.0, bias=two[:])
+                nc.scalar.activation(
+                    g[n][:], clipped[n][:], ACT.Identity, scale=minus_wt[:, n : n + 1], bias=wt_col[:, n : n + 1]
+                )
+            else:
+                nc.vector.tensor_scalar(clipped[n][:], err[n][:], 1.0, -1.0, ALU.min, ALU.max)
+                nc.scalar.activation(g[n][:], clipped[n][:], ACT.Copy, scale=wt_col[:, n : n + 1])
+            add_turned(db_sum, g[n], DB_ORDER.index(n))
+
+        def make_q(n):
             q = held.tile([P, SLOTS], F32, name=f"q{n}")
-            nc.vector.scalar_tensor_tensor(q[:], clipped[n][:], wu_col[:, n : n + 1], a_bank[n][:], ALU.mult, ALU.mult)
-            add_turned(ds_sum, q, n)
+            source, scale = (g[n], us_col) if n in ON_SCALAR else (clipped[n], wu_col)
+            nc.vector.scalar_tensor_tensor(q[:], source[:], scale[:, n : n + 1], a_bank[n][:], ALU.mult, ALU.mult)
+            add_turned(ds_sum, q, DS_ORDER.index(n))
+
+        def make_du(n):
             gta = held.tile([P, SLOTS], F32, name=f"gta{n}")
+            source, scale = (g[n], 1.0) if n in ON_SCALAR else (clipped[n], wt_col[:, n : n + 1])
             nc.vector.scalar_tensor_tensor(
-                gta[:],
-                clipped[n][:],
-                wt_col[:, n : n + 1],
-                ta[n][:],
-                ALU.mult,
-                ALU.mult,
-                accum_out=stats[:, 32 * n + 2 : 32 * n + 3],
+                gta[:], source[:], scale, ta[n][:], ALU.mult, ALU.mult, accum_out=stats[:, 32 * n + 2 : 32 * n + 3]
             )
 
-        front(0)
-        for n in range(1, TILES):
-            front(n)
-            back_half(n - 1)
-        back_half(TILES - 1)
+        DB_ORDER = [1, 0, 2, 3]
+        DS_ORDER = [0, 1, 3, 2]
+        make_ta(0)
+        make_ta(1)
+        make_err(0)
+        make_ta(2)
+        make_err(1)
+        make_ta(3)
+        make_err(2)
+        make_err(3)
+        clip(1)
+        clip(0)
+        clip(2)
+        make_q(0)
+        make_q(1)
+        clip(3)
+        make_du(0)
+        make_q(3)
+        make_du(1)
+        make_q(2)
+        make_du(3)
+        make_du(2)
 
         by_block = stats[:].rearrange("p (j c) -> p j c", c=32)
-        nc.vector.tensor_reduce(by_block[:, :, 1], db_sum[:], AXIS.X, ALU.add)
+        spent = held.tile([P, BLOCKS, P], F32, name="spent")
+        for j in range(BLOCKS):
+            nc.scalar.activation(spent[:, j, :], db_sum[:, j, :], ACT.Copy, accum_out=by_block[:, j, 1:2])
         nc.vector.tensor_reduce(by_block[:, :, 0], ds_sum[:], AXIS.X, ALU.add)
         rows = held.tile([P, P], F32, name="rows", align_bytes=64)
         nc.vector.transpose(rows[:], stats[:])

@@ -35,15 +35,15 @@ def tile_attend_gbias_s_hub_kernel(tc, xT, wT, ts, kb, us, y, wt, offs, out_0, o
         ts_row = held.tile([1, COLS], F32, name="ts_staged")
         kb_row = held.tile([1, COLS], F32, name="kb_staged")
         nc.sync.dma_start(ts_row[:], ts[0:1, :])
-        nc.sync.dma_start(kb_row[:], kb[0:1, :])
-
-        row_scales = held.tile([P, R], F32, name="row_scales")
-        nc.sync.dma_start(row_scales[32:33, :], us.rearrange("r o -> o r"))
-        nc.sync.dma_start(row_scales[64:65, :], wt.rearrange("r o -> o r"))
 
         w_rows = wT.rearrange("(p t) c -> t p c", t=PACK)
         w_plane = [held.tile([P, COLS], F32, name=f"w_plane{t}") for t in range(PACK)]
-        for t in range(PACK):
+        nc.sync.dma_start(w_plane[0][:], w_rows[0])
+        nc.sync.dma_start(kb_row[:], kb[0:1, :])
+        row_scales = held.tile([P, R], F32, name="row_scales")
+        nc.sync.dma_start(row_scales[32:33, :], us.rearrange("r o -> o r"))
+        nc.sync.dma_start(row_scales[64:65, :], wt.rearrange("r o -> o r"))
+        for t in range(1, PACK):
             nc.sync.dma_start(w_plane[t][:], w_rows[t])
 
         ts_window = held.tile([P, COLS], F32, name="ts_window")
@@ -90,23 +90,26 @@ def tile_attend_gbias_s_hub_kernel(tc, xT, wT, ts, kb, us, y, wt, offs, out_0, o
                 nc.tensor.transpose(back[:, j * P : (j + 1) * P], col[:, j : j + 1].to_broadcast([P, P]), ident[:])
             return back
 
-        ts_picked = gathered_row(ts_window, "ts")
+        ts_all = held.tile([P, SLOTS], F32, name="ts_all")
+        nc.scalar.copy(ts_all[:], spread(columns(gathered_row(ts_window, "ts"), "ts", 1)[:, 0, :], "ts", "ds_sum")[:])
+        kb_picked = gathered_row(kb_window, "kb")
         for part in (32, 64):
-            nc.scalar.copy(ts_picked[part : part + 1, :], row_scales[part : part + 1, :])
-        cols_held = columns(ts_picked, "ts", 3)
+            nc.scalar.copy(kb_picked[part : part + 1, :], row_scales[part : part + 1, :])
+        cols_held = columns(kb_picked, "kb", 3)
         us_col = cols_held[:, 1, :]
         wt_col = cols_held[:, 2, :]
-        ts_all = held.tile([P, SLOTS], F32, name="ts_all")
-        nc.scalar.copy(ts_all[:], spread(cols_held[:, 0, :], "ts", "ds_sum")[:])
-        kb_all = spread(columns(gathered_row(kb_window, "kb"), "kb", 1)[:, 0, :], "kb", "kb_all")
+        kb_all = spread(cols_held[:, 0, :], "kb", "kb_all")
         wu_col = held.tile([P, TILES], F32, name="wu_col")
         nc.gpsimd.tensor_tensor(wu_col[:], us_col, wt_col, ALU.mult)
         minus_wt = held.tile([P, TILES], F32, name="minus_wt")
         nc.gpsimd.tensor_scalar(minus_wt[:], wt_col, -1.0, 0.0, ALU.mult, ALU.add)
 
         w_words = held.tile([P, SLOTS, PACK], BF16, name="w_words", align_bytes=64)
-        for t in range(PACK - 1):
-            nc.vector.tensor_copy(w_words[:, :, t], w_plane[t][:].indirect(offsets[:]))
+        w_pair = held.tile([P, 2, SLOTS], BF16, name="w_pair")
+        for t in range(2):
+            nc.vector.tensor_copy(w_pair[:, t, :], w_plane[t][:].indirect(offsets[:]))
+        nc.scalar.copy(w_words[:, :, 0:2], w_pair[:].rearrange("p t s -> p s t"))
+        nc.vector.tensor_copy(w_words[:, :, 2], w_plane[2][:].indirect(offsets[:]))
         w_codes = held.tile([P, SLOTS], U32, name="w_codes", align_bytes=64)
         w_scales = held.tile([P, SLOTS], U8, name="w_scales", align_bytes=64)
         for h in range(2):
@@ -114,33 +117,45 @@ def tile_attend_gbias_s_hub_kernel(tc, xT, wT, ts, kb, us, y, wt, offs, out_0, o
                 w_words[:, h * HALF : (h + 1) * HALF, PACK - 1],
                 w_plane[PACK - 1][:].indirect(offsets[:, h * (HALF // 16) : (h + 1) * (HALF // 16)]),
             )
-        for h in range(2):
+
+        def quantise_w(h):
             cols = slice(h * HALF, (h + 1) * HALF)
             nc.vector.quantize_mx(
                 w_codes[:, cols].bitcast(FP8X4), w_scales[:, cols], w_words[:, cols, :].rearrange("p s t -> p (s t)")
             )
 
-        a_bank = []
-        for n in range(TILES):
+        x_codes = [held.tile([P, P], U32, name=f"x_codes{n}", align_bytes=64) for n in range(TILES)]
+        x_scales = [held.tile([P, P], U8, name=f"x_scales{n}", align_bytes=64) for n in range(TILES)]
+        a_bank = [psum.tile([P, SLOTS], F32, name=f"a_bank{n}") for n in range(TILES)]
+
+        def quantise_x(n):
             x_words = held.tile([P, P, PACK], BF16, name=f"x_words{n}", align_bytes=64)
             source = x_half[n // 2][:, :, (n % 2) * P : (n % 2 + 1) * P]
             nc.scalar.copy(
                 x_words[:].rearrange("p (c i) t -> p c t i", i=4), source.rearrange("p t (c i) -> p c t i", i=4)
             )
-            x_codes = held.tile([P, P], U32, name=f"x_codes{n}", align_bytes=64)
-            x_scales = held.tile([P, P], U8, name=f"x_scales{n}", align_bytes=64)
-            nc.vector.quantize_mx(x_codes[:].bitcast(FP8X4), x_scales[:], x_words[:].rearrange("p r t -> p (r t)"))
-            bank = psum.tile([P, SLOTS], F32, name=f"a_bank{n}")
+            nc.vector.quantize_mx(
+                x_codes[n][:].bitcast(FP8X4), x_scales[n][:], x_words[:].rearrange("p r t -> p (r t)")
+            )
+
+        def multiply(n, cols):
             nc.tensor.matmul_mx(
-                bank[:],
-                lhsT=x_codes[:].bitcast(FP8X4),
-                lhsT_scale=x_scales[:],
-                rhs=w_codes[:].bitcast(FP8X4),
-                rhs_scale=w_scales[:],
+                a_bank[n][:, cols],
+                lhsT=x_codes[n][:].bitcast(FP8X4),
+                lhsT_scale=x_scales[n][:],
+                rhs=w_codes[:, cols].bitcast(FP8X4),
+                rhs_scale=w_scales[:, cols],
                 start=True,
                 stop=True,
             )
-            a_bank.append(bank)
+
+        quantise_x(0)
+        for h in range(2):
+            quantise_w(h)
+            multiply(0, slice(h * HALF, (h + 1) * HALF))
+        for n in range(1, TILES):
+            quantise_x(n)
+            multiply(n, slice(0, SLOTS))
 
         ds_sum = psum.tile([P, BLOCKS, P], F32, name="ds_sum")
         db_sum = psum.tile([P, BLOCKS, P], F32, name="db_sum")
@@ -158,67 +173,65 @@ def tile_attend_gbias_s_hub_kernel(tc, xT, wT, ts, kb, us, y, wt, offs, out_0, o
 
         ta = [held.tile([P, SLOTS], F32, name=f"ta{n}") for n in range(TILES)]
         g = [held.tile([P, SLOTS], F32, name=f"g{n}") for n in range(TILES)]
-        clipped = [held.tile([P, SLOTS], F32, name=f"clipped{n}") for n in range(TILES)]
-        ON_SCALAR = (1, 2)
+        z_late = held.tile([P, 2, SLOTS], F32, name="z_late")
+        spent_du = held.tile([P, SLOTS], F32, name="spent_du")
+        spent_late = held.tile([P, SLOTS], F32, name="spent_late")
 
-        err = [held.tile([P, SLOTS], F32, name=f"err{n}") for n in range(TILES)]
+        def du_col(n):
+            return stats[:, 32 * n + 2 : 32 * n + 3]
 
         def make_ta(n):
             nc.vector.tensor_tensor(ta[n][:], a_bank[n][:], ts_all[:], ALU.mult)
 
-        def make_err(n):
+        def make_z(n, z):
+            nc.vector.scalar_tensor_tensor(z, ta[n][:], us_col[:, n : n + 1], kb_all[:], ALU.mult, ALU.add)
+
+        def early_g(n):
             z = held.tile([P, SLOTS], F32, name=f"z{n}")
-            nc.vector.scalar_tensor_tensor(z[:], ta[n][:], us_col[:, n : n + 1], kb_all[:], ALU.mult, ALU.add)
-            nc.gpsimd.tensor_tensor(err[n][:], z[:], y_half[n // 2][:, n % 2, :], ALU.subtract)
-
-        def clip(n):
-            if n in ON_SCALAR:
-                low = held.tile([P, SLOTS], F32, name=f"low{n}")
-                nc.scalar.activation(low[:], err[n][:], ACT.Relu, bias=one[:])
-                nc.scalar.activation(clipped[n][:], low[:], ACT.Relu, scale=-1.0, bias=two[:])
-                nc.scalar.activation(
-                    g[n][:], clipped[n][:], ACT.Identity, scale=minus_wt[:, n : n + 1], bias=wt_col[:, n : n + 1]
-                )
-            else:
-                nc.vector.tensor_scalar(clipped[n][:], err[n][:], 1.0, -1.0, ALU.min, ALU.max)
-                nc.scalar.activation(g[n][:], clipped[n][:], ACT.Copy, scale=wt_col[:, n : n + 1])
-            add_turned(db_sum, g[n], DB_ORDER.index(n))
-
-        def make_q(n):
-            q = held.tile([P, SLOTS], F32, name=f"q{n}")
-            source, scale = (g[n], us_col) if n in ON_SCALAR else (clipped[n], wu_col)
-            nc.vector.scalar_tensor_tensor(q[:], source[:], scale[:, n : n + 1], a_bank[n][:], ALU.mult, ALU.mult)
-            add_turned(ds_sum, q, DS_ORDER.index(n))
-
-        def make_du(n):
-            gta = held.tile([P, SLOTS], F32, name=f"gta{n}")
-            source, scale = (g[n], 1.0) if n in ON_SCALAR else (clipped[n], wt_col[:, n : n + 1])
-            nc.vector.scalar_tensor_tensor(
-                gta[:], source[:], scale, ta[n][:], ALU.mult, ALU.mult, accum_out=stats[:, 32 * n + 2 : 32 * n + 3]
+            make_z(n, z[:])
+            err = held.tile([P, SLOTS], F32, name=f"err{n}")
+            nc.gpsimd.tensor_tensor(err[:], z[:], y_half[0][:, n, :], ALU.subtract)
+            low = held.tile([P, SLOTS], F32, name=f"low{n}")
+            nc.scalar.activation(low[:], err[:], ACT.Relu, bias=one[:])
+            high = held.tile([P, SLOTS], F32, name=f"high{n}")
+            nc.scalar.activation(high[:], low[:], ACT.Relu, scale=-1.0, bias=two[:])
+            nc.scalar.activation(
+                g[n][:], high[:], ACT.Identity, scale=minus_wt[:, n : n + 1], bias=wt_col[:, n : n + 1]
             )
+            add_turned(db_sum, g[n], n)
 
-        DB_ORDER = [1, 0, 2, 3]
-        DS_ORDER = [0, 1, 3, 2]
+        def make_q(n, source, scale):
+            q = held.tile([P, SLOTS], F32, name=f"q{n}")
+            nc.vector.scalar_tensor_tensor(q[:], source, scale[:, n : n + 1], a_bank[n][:], ALU.mult, ALU.mult)
+            add_turned(ds_sum, q, n)
+
         make_ta(0)
         make_ta(1)
-        make_err(0)
+        early_g(0)
+        early_g(1)
         make_ta(2)
-        make_err(1)
         make_ta(3)
-        make_err(2)
-        make_err(3)
-        clip(1)
-        clip(0)
-        clip(2)
-        make_q(0)
-        make_q(1)
-        clip(3)
-        make_du(0)
-        make_q(3)
-        make_du(1)
-        make_q(2)
-        make_du(3)
-        make_du(2)
+        make_z(2, z_late[:, 0, :])
+        make_z(3, z_late[:, 1, :])
+        err_late = held.tile([P, 2, SLOTS], F32, name="err_late")
+        nc.vector.tensor_tensor(err_late[:], z_late[:], y_half[1][:], ALU.subtract)
+        clipped = held.tile([P, 2, SLOTS], F32, name="clipped")
+        nc.vector.tensor_scalar(clipped[:], err_late[:], 1.0, -1.0, ALU.min, ALU.max)
+        for n in (2, 3):
+            nc.scalar.activation(g[n][:], clipped[:, n - 2, :], ACT.Copy, scale=wt_col[:, n : n + 1])
+            add_turned(db_sum, g[n], n)
+        for n in (0, 1):
+            make_q(n, g[n][:], us_col)
+        for n in (2, 3):
+            make_q(n, clipped[:, n - 2, :], wu_col)
+        for n in (2, 3):
+            cta = held.tile([P, SLOTS], F32, name=f"cta{n}")
+            nc.gpsimd.tensor_tensor(cta[:], clipped[:, n - 2, :], ta[n][:], ALU.mult)
+            nc.scalar.activation(spent_late[:], cta[:], ACT.Copy, scale=wt_col[:, n : n + 1], accum_out=du_col(n))
+        for n in (0, 1):
+            nc.vector.scalar_tensor_tensor(
+                spent_du[:], g[n][:], 1.0, ta[n][:], ALU.mult, ALU.mult, accum_out=du_col(n)
+            )
 
         by_block = stats[:].rearrange("p (j c) -> p j c", c=32)
         spent = held.tile([P, BLOCKS, P], F32, name="spent")

@@ -60,10 +60,13 @@ def tile_attend_gbias_s_hub_kernel(tc, xT, wT, ts, kb, us, y, wt, offs, out_0, o
 
         x_rows = xT.rearrange("(p t) r -> p t r", t=PACK)
         y_rows = y.rearrange("(n p) i -> p n i", p=P)
-        x_half = [held.tile([P, PACK, HALF], F32, name=f"x_half{h}") for h in range(2)]
+        x_tile = []
+        for first, count in ((0, 1), (1, 1), (2, 2)):
+            piece = held.tile([P, PACK, count * P], F32, name=f"x_piece{first}")
+            nc.sync.dma_start(piece[:], x_rows[:, :, first * P : (first + count) * P])
+            x_tile.extend(piece[:, :, c * P : (c + 1) * P] for c in range(count))
         y_half = [held.tile([P, 2, SLOTS], F32, name=f"y_half{h}") for h in range(2)]
         for h in range(2):
-            nc.sync.dma_start(x_half[h][:], x_rows[:, :, h * HALF : (h + 1) * HALF])
             nc.sync.dma_start(y_half[h][:], y_rows[:, 2 * h : 2 * h + 2, :])
 
         ident = held.tile([P, P], F32, name="ident")
@@ -130,7 +133,7 @@ def tile_attend_gbias_s_hub_kernel(tc, xT, wT, ts, kb, us, y, wt, offs, out_0, o
 
         def quantise_x(n):
             x_words = held.tile([P, P, PACK], BF16, name=f"x_words{n}", align_bytes=64)
-            source = x_half[n // 2][:, :, (n % 2) * P : (n % 2 + 1) * P]
+            source = x_tile[n]
             nc.scalar.copy(
                 x_words[:].rearrange("p (c i) t -> p c t i", i=4), source.rearrange("p t (c i) -> p c t i", i=4)
             )
@@ -138,9 +141,15 @@ def tile_attend_gbias_s_hub_kernel(tc, xT, wT, ts, kb, us, y, wt, offs, out_0, o
                 x_codes[n][:].bitcast(FP8X4), x_scales[n][:], x_words[:].rearrange("p r t -> p (r t)")
             )
 
-        def multiply(n, cols):
+        a_first = psum.tile([P, HALF], F32, name="a_first", tag="turned")
+        halves = [slice(h * HALF, (h + 1) * HALF) for h in range(2)]
+        a_parts = [[(a_first[:], halves[0]), (a_bank[0][:, 0:HALF], halves[1])]]
+        a_parts.extend([(a_bank[n][:], slice(0, SLOTS))] for n in range(1, TILES))
+
+        def multiply(n, part):
+            target, cols = a_parts[n][part]
             nc.tensor.matmul_mx(
-                a_bank[n][:, cols],
+                target,
                 lhsT=x_codes[n][:].bitcast(FP8X4),
                 lhsT_scale=x_scales[n][:],
                 rhs=w_codes[:, cols].bitcast(FP8X4),
@@ -152,10 +161,10 @@ def tile_attend_gbias_s_hub_kernel(tc, xT, wT, ts, kb, us, y, wt, offs, out_0, o
         quantise_x(0)
         for h in range(2):
             quantise_w(h)
-            multiply(0, slice(h * HALF, (h + 1) * HALF))
+            multiply(0, h)
         for n in range(1, TILES):
             quantise_x(n)
-            multiply(n, slice(0, SLOTS))
+            multiply(n, 0)
 
         ds_sum = psum.tile([P, BLOCKS, P], F32, name="ds_sum")
         db_sum = psum.tile([P, BLOCKS, P], F32, name="db_sum")
@@ -181,10 +190,14 @@ def tile_attend_gbias_s_hub_kernel(tc, xT, wT, ts, kb, us, y, wt, offs, out_0, o
             return stats[:, 32 * n + 2 : 32 * n + 3]
 
         def make_ta(n):
-            nc.vector.tensor_tensor(ta[n][:], a_bank[n][:], ts_all[:], ALU.mult)
+            for a, cols in a_parts[n]:
+                nc.vector.tensor_tensor(ta[n][:, cols], a, ts_all[:, cols], ALU.mult)
 
         def make_z(n, z):
-            nc.vector.scalar_tensor_tensor(z, ta[n][:], us_col[:, n : n + 1], kb_all[:], ALU.mult, ALU.add)
+            for a, cols in a_parts[n]:
+                nc.vector.scalar_tensor_tensor(
+                    z[:, cols], ta[n][:, cols], us_col[:, n : n + 1], kb_all[:, cols], ALU.mult, ALU.add
+                )
 
         def early_g(n):
             z = held.tile([P, SLOTS], F32, name=f"z{n}")
@@ -202,33 +215,35 @@ def tile_attend_gbias_s_hub_kernel(tc, xT, wT, ts, kb, us, y, wt, offs, out_0, o
 
         def make_q(n, source, scale):
             q = held.tile([P, SLOTS], F32, name=f"q{n}")
-            nc.vector.scalar_tensor_tensor(q[:], source, scale[:, n : n + 1], a_bank[n][:], ALU.mult, ALU.mult)
+            for a, cols in a_parts[n]:
+                nc.vector.scalar_tensor_tensor(q[:, cols], source[:, cols], scale[:, n : n + 1], a, ALU.mult, ALU.mult)
             add_turned(ds_sum, q, n)
 
         make_ta(0)
-        make_ta(1)
         early_g(0)
-        early_g(1)
+        make_ta(1)
         make_ta(2)
+        early_g(1)
         make_ta(3)
-        make_z(2, z_late[:, 0, :])
-        make_z(3, z_late[:, 1, :])
         err_late = held.tile([P, 2, SLOTS], F32, name="err_late")
-        nc.vector.tensor_tensor(err_late[:], z_late[:], y_half[1][:], ALU.subtract)
+        make_z(2, z_late[:, 0, :])
+        nc.gpsimd.tensor_tensor(err_late[:, 0, :], z_late[:, 0, :], y_half[1][:, 0, :], ALU.subtract)
+        make_z(3, z_late[:, 1, :])
+        make_q(0, g[0][:], us_col)
+        nc.vector.tensor_tensor(err_late[:, 1, :], z_late[:, 1, :], y_half[1][:, 1, :], ALU.subtract)
+        make_q(1, g[1][:], us_col)
         clipped = held.tile([P, 2, SLOTS], F32, name="clipped")
         nc.vector.tensor_scalar(clipped[:], err_late[:], 1.0, -1.0, ALU.min, ALU.max)
         for n in (2, 3):
             nc.scalar.activation(g[n][:], clipped[:, n - 2, :], ACT.Copy, scale=wt_col[:, n : n + 1])
             add_turned(db_sum, g[n], n)
-        for n in (0, 1):
-            make_q(n, g[n][:], us_col)
         for n in (2, 3):
             make_q(n, clipped[:, n - 2, :], wu_col)
-        for n in (2, 3):
+        for n in (2,):
             cta = held.tile([P, SLOTS], F32, name=f"cta{n}")
             nc.gpsimd.tensor_tensor(cta[:], clipped[:, n - 2, :], ta[n][:], ALU.mult)
             nc.scalar.activation(spent_late[:], cta[:], ACT.Copy, scale=wt_col[:, n : n + 1], accum_out=du_col(n))
-        for n in (0, 1):
+        for n in (0, 1, 3):
             nc.vector.scalar_tensor_tensor(
                 spent_du[:], g[n][:], 1.0, ta[n][:], ALU.mult, ALU.mult, accum_out=du_col(n)
             )

from contextlib import ExitStack

import concourse.mybir as mybir
from concourse.masks import make_identity

F32 = mybir.dt.float32
BF16 = mybir.dt.bfloat16
U32 = mybir.dt.uint32
U16 = mybir.dt.uint16
U8 = mybir.dt.uint8
FP8X4 = mybir.dt.float8_e4m3fn_x4
ALU = mybir.AluOpType
ACT = mybir.ActivationFunctionType
AXIS = mybir.AxisListType

P = 128
PACK = 4
D, R, SLOTS, COLS = 512, 512, 512, 2048
TILES = R // P
BLOCKS = SLOTS // P
HALF = 256
FLOPS = 2 * D * R * SLOTS
BYTES = 4 * (D * R + D * COLS + 2 * COLS + 2 * R + R * SLOTS + 2 * SLOTS + R) + 2 * 128 * 32


def tile_attend_gbias_s_hub_kernel(tc, xT, wT, ts, kb, us, y, wt, offs, out_0, out_1, out_2):
    nc = tc.nc
    with ExitStack() as ctx:
        held = ctx.enter_context(tc.tile_pool(name="held", bufs=1))
        psum = ctx.enter_context(tc.psum_pool(name="psum", bufs=1))

        offsets = held.tile([P, SLOTS // 16], U16, name="offsets")
        nc.sync.dma_start(offsets[:], offs)

        ts_row = held.tile([1, COLS], F32, name="ts_staged")
        kb_row = held.tile([1, COLS], F32, name="kb_staged")
        nc.sync.dma_start(ts_row[:], ts[0:1, :])

        w_rows = wT.rearrange("(p t) c -> t p c", t=PACK)
        w_plane = [held.tile([P, COLS], F32, name=f"w_plane{t}") for t in range(PACK)]
        nc.sync.dma_start(w_plane[0][:], w_rows[0])
        nc.sync.dma_start(kb_row[:], kb[0:1, :])
        row_scales = held.tile([P, R], F32, name="row_scales")
        nc.sync.dma_start(row_scales[32:33, :], us.rearrange("r o -> o r"))
        nc.sync.dma_start(row_scales[64:65, :], wt.rearrange("r o -> o r"))
        for t in range(1, PACK):
            nc.sync.dma_start(w_plane[t][:], w_rows[t])

        ts_window = held.tile([P, COLS], F32, name="ts_window")
        kb_window = held.tile([P, COLS], F32, name="kb_window")
        one = held.tile([P, 1], F32, name="one")
        two = held.tile([P, 1], F32, name="two")
        nc.gpsimd.memset(one[:], 1.0)
        nc.scalar.activation(two[:], one[:], ACT.Identity, bias=one[:])
        nc.vector.memset(ts_window[:], 0.0)
        nc.gpsimd.memset(kb_window[:], 0.0)
        nc.vector.tensor_copy(ts_window[0:1, :], ts_row[:])
        nc.scalar.activation(kb_window[0:1, :], kb_row[:], ACT.Copy)


        x_rows = xT.rearrange("(p t) r -> p t r", t=PACK)
        y_rows = y.rearrange("(n p) i -> p n i", p=P)
        x_tile = []
        for first, count in ((0, 1), (1, 1), (2, 2)):
            piece = held.tile([P, PACK, count * P], F32, name=f"x_piece{first}")
            nc.sync.dma_start(piece[:], x_rows[:, :, first * P : (first + count) * P])
            x_tile.extend(piece[:, :, c * P : (c + 1) * P] for c in range(count))
        y_half = [held.tile([P, 2, SLOTS], F32, name=f"y_half{h}") for h in range(2)]
        for h in range(2):
            nc.sync.dma_start(y_half[h][:], y_rows[:, 2 * h : 2 * h + 2, :])

        ident = held.tile([P, P], F32, name="ident")
        make_identity(nc, ident[:])
        stats = held.tile([P, P], F32, name="stats", align_bytes=64)
        nc.gpsimd.memset(stats[:], 0.0)

        def gathered_row(window, name):
            row = held.tile([P, SLOTS], F32, name=name + "_row")
            nc.vector.tensor_copy(row[:], window[:].indirect(offsets[:]))
            return row

        def columns(row, name, picked):
            turned = psum.tile([P, BLOCKS, P], F32, name=name + "_turned", tag="turned")
            for j in range(BLOCKS):
                nc.tensor.transpose(turned[:, j, :], row[:, j * P : (j + 1) * P], ident[:])
            col = held.tile([P, picked, BLOCKS], F32, name=name + "_col")
            nc.scalar.copy(col[:], turned[:, :, 0 : 32 * picked : 32].rearrange("p j c -> p c j"))
            return col

        def spread(col, name, tag):
            back = psum.tile([P, SLOTS], F32, name=name + "_back", tag=tag)
            for j in range(BLOCKS):
                nc.tensor.transpose(back[:, j * P : (j + 1) * P], col[:, j : j + 1].to_broadcast([P, P]), ident[:])
            return back

        ts_all = held.tile([P, SLOTS], F32, name="ts_all")
        nc.scalar.copy(ts_all[:], spread(columns(gathered_row(ts_window, "ts"), "ts", 1)[:, 0, :], "ts", "ds_sum")[:])
        kb_picked = gathered_row(kb_window, "kb")
        for part in (32, 64):
            nc.scalar.copy(kb_picked[part : part + 1, :], row_scales[part : part + 1, :])
        cols_held = columns(kb_picked, "kb", 3)
        us_col = cols_held[:, 1, :]
        wt_col = cols_held[:, 2, :]
        kb_all = spread(cols_held[:, 0, :], "kb", "kb_all")
        wu_col = held.tile([P, TILES], F32, name="wu_col")
        nc.gpsimd.tensor_tensor(wu_col[:], us_col, wt_col, ALU.mult)
        minus_wt = held.tile([P, TILES], F32, name="minus_wt")
        nc.gpsimd.tensor_scalar(minus_wt[:], wt_col, -1.0, 0.0, ALU.mult, ALU.add)

        w_words = held.tile([P, SLOTS, PACK], BF16, name="w_words", align_bytes=64)
        w_pair = held.tile([P, 2, SLOTS], BF16, name="w_pair")
        for t in range(2):
            nc.vector.tensor_copy(w_pair[:, t, :], w_plane[t][:].indirect(offsets[:]))
        nc.scalar.copy(w_words[:, :, 0:2], w_pair[:].rearrange("p t s -> p s t"))
        nc.vector.tensor_copy(w_words[:, :, 2], w_plane[2][:].indirect(offsets[:]))
        w_codes = held.tile([P, SLOTS], U32, name="w_codes", align_bytes=64)
        w_scales = held.tile([P, SLOTS], U8, name="w_scales", align_bytes=64)
        for h in range(2):
            nc.vector.tensor_copy(
                w_words[:, h * HALF : (h + 1) * HALF, PACK - 1],
                w_plane[PACK - 1][:].indirect(offsets[:, h * (HALF // 16) : (h + 1) * (HALF // 16)]),
            )

        def quantise_w(h):
            cols = slice(h * HALF, (h + 1) * HALF)
            nc.vector.quantize_mx(
                w_codes[:, cols].bitcast(FP8X4), w_scales[:, cols], w_words[:, cols, :].rearrange("p s t -> p (s t)")
            )

        x_codes = [held.tile([P, P], U32, name=f"x_codes{n}", align_bytes=64) for n in range(TILES)]
        x_scales = [held.tile([P, P], U8, name=f"x_scales{n}", align_bytes=64) for n in range(TILES)]
        a_bank = [psum.tile([P, SLOTS], F32, name=f"a_bank{n}") for n in range(TILES)]

        def quantise_x(n):
            x_words = held.tile([P, P, PACK], BF16, name=f"x_words{n}", align_bytes=64)
            source = x_tile[n]
            nc.scalar.copy(
                x_words[:].rearrange("p (c i) t -> p c t i", i=4), source.rearrange("p t (c i) -> p c t i", i=4)
            )
            nc.vector.quantize_mx(
                x_codes[n][:].bitcast(FP8X4), x_scales[n][:], x_words[:].rearrange("p r t -> p (r t)")
            )

        a_first = psum.tile([P, HALF], F32, name="a_first", tag="turned")
        halves = [slice(h * HALF, (h + 1) * HALF) for h in range(2)]
        a_parts = [[(a_first[:], halves[0]), (a_bank[0][:, 0:HALF], halves[1])]]
        a_parts.extend([(a_bank[n][:], slice(0, SLOTS))] for n in range(1, TILES))

        def multiply(n, part):
            target, cols = a_parts[n][part]
            nc.tensor.matmul_mx(
                target,
                lhsT=x_codes[n][:].bitcast(FP8X4),
                lhsT_scale=x_scales[n][:],
                rhs=w_codes[:, cols].bitcast(FP8X4),
                rhs_scale=w_scales[:, cols],
                start=True,
                stop=True,
            )

        quantise_x(0)
        for h in range(2):
            quantise_w(h)
            multiply(0, h)
        for n in range(1, TILES):
            quantise_x(n)
            multiply(n, 0)

        ds_sum = psum.tile([P, BLOCKS, P], F32, name="ds_sum")
        db_sum = psum.tile([P, BLOCKS, P], F32, name="db_sum")

        def add_turned(total, tile, n):
            for j in range(BLOCKS):
                nc.tensor.matmul(
                    total[:, j, :],
                    lhsT=tile[:, j * P : (j + 1) * P],
                    rhs=ident[:],
                    is_transpose=True,
                    start=(n == 0 and j == 0),
                    stop=(n == TILES - 1 and j == BLOCKS - 1),
                )

        ta = [held.tile([P, SLOTS], F32, name=f"ta{n}") for n in range(TILES)]
        g = [held.tile([P, SLOTS], F32, name=f"g{n}") for n in range(TILES)]
        z_late = held.tile([P, 2, SLOTS], F32, name="z_late")
        spent_du = held.tile([P, SLOTS], F32, name="spent_du")
        spent_late = held.tile([P, SLOTS], F32, name="spent_late")

        def du_col(n):
            return stats[:, 32 * n + 2 : 32 * n + 3]

        def make_ta(n):
            for a, cols in a_parts[n]:
                nc.vector.tensor_tensor(ta[n][:, cols], a, ts_all[:, cols], ALU.mult)

        def make_z(n, z):
            for a, cols in a_parts[n]:
                nc.vector.scalar_tensor_tensor(
                    z[:, cols], ta[n][:, cols], us_col[:, n : n + 1], kb_all[:, cols], ALU.mult, ALU.add
                )

        def early_g(n):
            z = held.tile([P, SLOTS], F32, name=f"z{n}")
            make_z(n, z[:])
            err = held.tile([P, SLOTS], F32, name=f"err{n}")
            nc.gpsimd.tensor_tensor(err[:], z[:], y_half[0][:, n, :], ALU.subtract)
            low = held.tile([P, SLOTS], F32, name=f"low{n}")
            nc.scalar.activation(low[:], err[:], ACT.Relu, bias=one[:])
            high = held.tile([P, SLOTS], F32, name=f"high{n}")
            nc.scalar.activation(high[:], low[:], ACT.Relu, scale=-1.0, bias=two[:])
            nc.scalar.activation(
                g[n][:], high[:], ACT.Identity, scale=minus_wt[:, n : n + 1], bias=wt_col[:, n : n + 1]
            )
            add_turned(db_sum, g[n], n)

        def make_q(n, source, scale):
            q = held.tile([P, SLOTS], F32, name=f"q{n}")
            for a, cols in a_parts[n]:
                nc.vector.scalar_tensor_tensor(q[:, cols], source[:, cols], scale[:, n : n + 1], a, ALU.mult, ALU.mult)
            add_turned(ds_sum, q, n)

        make_ta(0)
        early_g(0)
        make_ta(1)
        make_ta(2)
        early_g(1)
        make_ta(3)
        err_late = held.tile([P, 2, SLOTS], F32, name="err_late")
        make_z(2, z_late[:, 0, :])
        nc.gpsimd.tensor_tensor(err_late[:, 0, :], z_late[:, 0, :], y_half[1][:, 0, :], ALU.subtract)
        make_z(3, z_late[:, 1, :])
        make_q(0, g[0][:], us_col)
        nc.vector.tensor_tensor(err_late[:, 1, :], z_late[:, 1, :], y_half[1][:, 1, :], ALU.subtract)
        make_q(1, g[1][:], us_col)
        clipped = held.tile([P, 2, SLOTS], F32, name="clipped")
        nc.vector.tensor_scalar(clipped[:], err_late[:], 1.0, -1.0, ALU.min, ALU.max)
        for n in (2, 3):
            nc.scalar.activation(g[n][:], clipped[:, n - 2, :], ACT.Copy, scale=wt_col[:, n : n + 1])
            add_turned(db_sum, g[n], n)
        for n in (2, 3):
            make_q(n, clipped[:, n - 2, :], wu_col)
        for n in (2,):
            cta = held.tile([P, SLOTS], F32, name=f"cta{n}")
            nc.gpsimd.tensor_tensor(cta[:], clipped[:, n - 2, :], ta[n][:], ALU.mult)
            nc.scalar.activation(spent_late[:], cta[:], ACT.Copy, scale=wt_col[:, n : n + 1], accum_out=du_col(n))
        for n in (0, 1, 3):
            nc.vector.scalar_tensor_tensor(
                spent_du[:], g[n][:], 1.0, ta[n][:], ALU.mult, ALU.mult, accum_out=du_col(n)
            )

        by_block = stats[:].rearrange("p (j c) -> p j c", c=32)
        spent = held.tile([P, BLOCKS, P], F32, name="spent")
        for j in range(BLOCKS):
            nc.scalar.activation(spent[:, j, :], db_sum[:, j, :], ACT.Copy, accum_out=by_block[:, j, 1:2])
        nc.vector.tensor_reduce(by_block[:, :, 0], ds_sum[:], AXIS.X, ALU.add)
        rows = held.tile([P, P], F32, name="rows", align_bytes=64)
        nc.vector.transpose(rows[:], stats[:])
        for o, (out, queue) in enumerate(((out_0, nc.sync), (out_1, nc.scalar), (out_2, nc.sync))):
            queue.dma_start(
                out.rearrange("o (j b k) -> b (o j) k", b=4, k=32),
                rows[o:P:32, :].rearrange("b (j k) -> b j k", k=32),
            )
